import numpy as np
import ml_dtypes


def mxq(x, axis, fmt="e4m3"):
    dtype, down = {"e4m3": (ml_dtypes.float8_e4m3fn, 7), "e5m2": (ml_dtypes.float8_e5m2, 14)}[fmt]
    v = np.moveaxis(np.asarray(x, np.float32).astype(ml_dtypes.bfloat16).astype(np.float64), axis, -1)
    blocks = v.reshape(v.shape[:-1] + (-1, 32))
    amax = np.abs(blocks).max(-1, keepdims=True)
    byte = np.maximum(np.where(amax > 0, np.frexp(amax)[1] - 1 + 127, 0) - down, 1)
    scale = np.exp2(byte - 127.0)
    codes = (blocks / scale).astype(np.float32).astype(dtype).astype(np.float64)
    return np.moveaxis((codes * scale).reshape(v.shape), -1, axis)


WIDE = False


def mx_kscale(k):
    if not WIDE:
        return np.ones(k)
    levels = np.array([30, -30])
    if k % 512:
        return np.exp2(np.random.permutation(np.resize(levels, k // 32))).repeat(32)
    a = np.empty((k // 512, 16))
    for p in range(k // 512):
        a[p, :8] = np.random.permutation(np.resize(levels, 8))
        for g in range(8):
            far = levels[np.abs(levels - a[p, g]) >= 10]
            a[p, g + 8] = far[np.random.randint(len(far))]
    return np.exp2(a.ravel()).repeat(32)


def f64(x):
    return np.asarray(x).astype(np.float64)


def striped(idx):
    return np.tile(np.asarray(idx).reshape(-1, 16).T, (8, 1)).astype(np.uint16)


def unstriped(offs):
    return offs[:16].T.reshape(-1).astype(np.int64)


E2M1 = np.array([0.0, 0.5, 1.0, 1.5, 2.0, 3.0, 4.0, 6.0, -0.0, -0.5, -1.0, -1.5, -2.0, -3.0, -4.0, -6.0])


def pack_weight(w, fmt):
    k, n = w.shape
    w = f64(np.asarray(w, np.float32).astype(ml_dtypes.bfloat16)).reshape(k // 32, 32, n)
    amax = np.abs(w).max(1)
    if fmt in ("e4m3", "e5m2"):
        byte = np.frexp(amax)[1] - 1 + 127 - (7 if fmt == "e4m3" else 14)
    else:
        mant, ex = np.frexp(amax / 6.0)
        byte = np.where(mant > 0.5, ex, ex - 1) + 127
    byte = np.clip(np.where(amax > 0, byte, 1), 1, 254)
    scaled = (w * np.exp2(127.0 - byte)[:, None, :]).reshape(k, n).astype(np.float32)
    by_word = np.ascontiguousarray(scaled.reshape(k // 512, 128, 4, n).transpose(0, 1, 3, 2))
    if fmt in ("e4m3", "e5m2"):
        words = by_word.astype(ml_dtypes.float8_e4m3fn if fmt == "e4m3" else ml_dtypes.float8_e5m2).view(np.uint8)
    else:
        c = by_word.astype(ml_dtypes.float4_e2m1fn).view(np.uint8) & 0xF
        words = (c[..., 0::2] | (c[..., 1::2] << 4)).reshape(k // 512, 128, 2 * n)
    return np.ascontiguousarray(words), np.ascontiguousarray(byte.astype(np.uint8).reshape(k // 512, 16, n))


def unpack_weight(words, scales, fmt):
    g, _, n = scales.shape
    words = np.ascontiguousarray(words).reshape(g, 128, n, -1)
    if fmt in ("e4m3", "e5m2"):
        vals = words.view(ml_dtypes.float8_e4m3fn if fmt == "e4m3" else ml_dtypes.float8_e5m2).astype(np.float64)
    else:
        nib = np.empty((g, 128, n, 4), np.uint8)
        nib[..., 0::2] = words & 0xF
        nib[..., 1::2] = words >> 4
        vals = E2M1[nib]
    vals = vals * np.repeat(np.exp2(scales.astype(np.float64) - 127.0), 8, axis=1)[..., None]
    return vals.transpose(0, 1, 3, 2).reshape(g * 512, n)


K, T, J, R, G, N, E = 1024, 1024, 256, 512, 32, 256, 64


def setup_inputs():
    n = np.random.standard_normal
    idx = np.random.permutation(T)[:J]
    idx2 = np.random.permutation(J)[:E]
    idx3 = np.random.permutation(J)[:E]
    fk = mx_kscale(K)
    fr = mx_kscale(R)
    wp = pack_weight(n((K, R)) * 1 / np.sqrt(K) * fk[:, None] * fr, "e2m1")
    wbp = pack_weight(n((R, N)) * 1 / np.sqrt(R) / fr[:, None], "e5m2")
    return {
        "xf": (n((K, T))).astype(np.float32),
        "fk": (np.random.uniform(0.5, 2.0, (K, 1)) / fk[:, None]).astype(np.float32),
        "w_words": wp[0],
        "w_scales": wp[1],
        "wb_words": wbp[0],
        "wb_scales": wbp[1],
        "gm": (np.random.uniform(0.5, 2.0, (N, 1))).astype(np.float32),
        "offs": striped(idx),
        "offs2": striped(idx2),
        "offs3": striped(idx3),
    }


def reference(xf, fk, w_words, w_scales, wb_words, wb_scales, gm, offs, offs2, offs3):
    idx = unstriped(offs)
    idx2 = unstriped(offs2)
    idx3 = unstriped(offs3)
    wu = unpack_weight(w_words, w_scales, "e2m1")
    wbu = unpack_weight(wb_words, wb_scales, "e5m2")
    xg = f64(xf)[:, idx]
    x1 = np.pad(xg, ((0, 0), (1, 0)))[:, :J]
    u = (xg - 0.6 * x1) * f64(fk)
    uq = mxq(u, 0, "e4m3")
    a = wu.T @ uq
    m1 = a.reshape(R, G, J // G).mean(axis=2)
    m2 = np.repeat(m1, J // G, axis=1)
    hid = a - m2
    hidq = mxq(hid, 0, "e5m2")
    p = wbu.T @ hidq
    y = (p[:, idx2] - p[:, idx3]) * f64(gm)
    return y

@@ -1,0 +1,219 @@
+from contextlib import ExitStack
+
+import concourse.mybir as mybir
+
+K, T, J, R, N, E = 1024, 1024, 256, 512, 256, 64
+BUNDLE = 8
+FLOPS = 2 * K * R * J + 2 * R * N * J
+
+F32 = mybir.dt.float32
+BF16 = mybir.dt.bfloat16
+I32 = mybir.dt.int32
+U32 = mybir.dt.uint32
+U16 = mybir.dt.uint16
+U8 = mybir.dt.uint8
+E4M3 = mybir.dt.float8_e4m3fn_x4
+E5M2 = mybir.dt.float8_e5m2_x4
+E2M1 = mybir.dt.float4_e2m1fn_x4
+ALU = mybir.AluOpType
+COPY = mybir.ActivationFunctionType.Copy
+
+P = 128
+PACK = 4
+PASSES = K // (P * PACK)
+HALF = J // 2
+PAD = 8
+
+
+def tile_list_steps_levelled_pickgap_kernel(tc, xf, fk, w_words, w_scales, wb_words, wb_scales, gm, offs, offs2, offs3, out):
+    nc = tc.nc
+    with ExitStack() as ctx:
+        sb = ctx.enter_context(tc.tile_pool(name="sb", bufs=1))
+        ps = ctx.enter_context(tc.psum_pool(name="ps", bufs=1))
+
+        def tile(shape, dtype, name):
+            return sb.tile(shape, dtype, name=name, align_bytes=64)
+
+        slots = tile([P, J // 16], U16, "slots")
+        firsts = tile([P, E // 16], U16, "firsts")
+        seconds = tile([P, E // 16], U16, "seconds")
+        planes = [tile([P, T], F32, "plane%d" % i) for i in range(PASSES * PACK)]
+        fk_sb = tile([P, PASSES, 8], F32, "fk_sb")
+        gm_sb = tile([P, 2, 8], F32, "gm_sb")
+        w_raw = tile([P, PASSES, 2 * R], U8, "w_raw")
+        ws_raw = tile([P, PASSES, R], U8, "ws_raw")
+        w_sb = tile([P, PASSES, 2 * R], U8, "w_sb")
+        ws_sb = tile([P, PASSES, R], U8, "ws_sb")
+        wb_sb = tile([P, N], U32, "wb_sb")
+        wbs_sb = tile([P, N], U8, "wbs_sb")
+        picked = [tile([P, PAD + J], F32, "picked%d" % i) for i in range(PASSES * PACK)]
+
+        nc.gpsimd.memset(ws_raw[:].bitcast(I32), 0)
+        for g in picked:
+            nc.gpsimd.memset(g[:, 0:PAD], 0.0)
+        nc.gpsimd.memset(wbs_sb[:].bitcast(I32), 0)
+
+        x_rows = xf.rearrange("(a p i) t -> a i p t", a=PASSES, i=PACK)
+
+        def load_plane(i):
+            nc.sync.dma_start(out=planes[i][:], in_=x_rows[i // PACK, i % PACK])
+
+        load_plane(0)
+        nc.sync.dma_start(slots[:], offs)
+        nc.sync.dma_start(out=w_raw[:].bitcast(I32), in_=w_words.rearrange("a p c -> p a c").bitcast(I32))
+        load_plane(1)
+        nc.sync.dma_start(out=fk_sb[:, :, 0:PACK], in_=fk.rearrange("(a p i) o -> p a (i o)", a=PASSES, i=PACK))
+        for q in range(4):
+            nc.sync.dma_start(
+                out=ws_raw[32 * q : 32 * q + 4, :, :].bitcast(I32),
+                in_=w_scales[:, 4 * q : 4 * q + 4, :].rearrange("a r c -> r a c").bitcast(I32),
+            )
+        for i in range(2, PASSES * PACK):
+            load_plane(i)
+        nc.sync.dma_start(out=wb_sb[:].bitcast(I32), in_=wb_words[0].rearrange("p n t -> p (n t)").bitcast(I32))
+        for q in range(4):
+            nc.sync.dma_start(
+                out=wbs_sb[32 * q : 32 * q + 4, :].bitcast(I32),
+                in_=wb_scales[0, 4 * q : 4 * q + 4, :].bitcast(I32),
+            )
+        with nc.allow_non_contiguous_dma(reason="one factor a partition"):
+            nc.sync.dma_start(out=gm_sb[:, :, 0:1], in_=gm.rearrange("(c m) o -> m c o", c=2))
+        nc.sync.dma_start(firsts[:], offs2)
+        nc.sync.dma_start(seconds[:], offs3)
+
+        for a in range(PASSES):
+            nc.vector.tensor_copy(
+                out=w_sb[:, a, :].bitcast(U16).rearrange("p (t m) -> p t m", t=PACK),
+                in_=w_raw[:, a, :].bitcast(U16).rearrange("p (m t) -> p t m", t=PACK),
+            )
+            nc.vector.tensor_copy(
+                out=ws_sb[:, a, :].rearrange("p (t m) -> p t m", t=PACK),
+                in_=ws_raw[:, a, :].rearrange("p (m t) -> p t m", t=PACK),
+            )
+
+        steps = [tile([P, J], F32, "steps%d" % i) for i in range(PASSES * PACK)]
+        u_bf = [tile([P, J, PACK], BF16, "u_bf%d" % a) for a in range(PASSES)]
+        u_codes = [tile([P, J], U32, "u_codes%d" % a) for a in range(PASSES)]
+        u_scales = [tile([P, J], U8, "u_scales%d" % a) for a in range(PASSES)]
+        a_banks = [ps.tile([P, PACK, HALF], F32, name="a_bank%d" % h) for h in range(2)]
+
+        def step_and_round(i, lo, hi):
+            a, t = divmod(i, PACK)
+            nc.vector.scalar_tensor_tensor(
+                out=steps[i][:, lo:hi],
+                in0=picked[i][:, PAD - 1 + lo : PAD - 1 + hi],
+                scalar=-0.6,
+                in1=picked[i][:, PAD + lo : PAD + hi],
+                op0=ALU.mult,
+                op1=ALU.add,
+            )
+            nc.vector.tensor_scalar(
+                out=u_bf[a][:, lo:hi, t],
+                in0=steps[i][:, lo:hi],
+                scalar1=fk_sb[:, a, t : t + 1],
+                scalar2=None,
+                op0=ALU.mult,
+            )
+
+        def first_product(a, h):
+            cols = slice(h * HALF, (h + 1) * HALF)
+            nc.vector.quantize_mx(
+                out=u_codes[a][:, cols].bitcast(E4M3),
+                scales=u_scales[a][:, cols],
+                in_=u_bf[a][:, cols, :].rearrange("p j t -> p (j t)"),
+            )
+            for t in range(PACK):
+                nc.tensor.matmul_mx(
+                    out=a_banks[h][:, t, :],
+                    lhsT=w_sb[:, a, 2 * P * t : 2 * P * (t + 1)].bitcast(E2M1),
+                    lhsT_scale=ws_sb[:, a, P * t : P * (t + 1)],
+                    rhs=u_codes[a][:, cols].bitcast(E4M3),
+                    rhs_scale=u_scales[a][:, cols],
+                    start=(a == 0 and t == 0),
+                    stop=(a == PASSES - 1 and t == PACK - 1),
+                )
+
+        last = PASSES * PACK - 1
+        for i in range(last):
+            nc.scalar.activation(picked[i][:, PAD:], planes[i][:].indirect(slots[:]), COPY)
+            step_and_round(i, 0, J)
+            if i == PACK - 1:
+                first_product(0, 0)
+                first_product(0, 1)
+        nc.vector.tensor_copy(picked[last][:, PAD : PAD + HALF], planes[last][:].indirect(slots[:, 0 : HALF // 16]))
+        nc.scalar.activation(picked[last][:, PAD + HALF :], planes[last][:].indirect(slots[:, HALF // 16 :]), COPY)
+        for h in range(2):
+            step_and_round(last, h * HALF, (h + 1) * HALF)
+            first_product(PASSES - 1, h)
+
+        gm_wide = tile([P, 2, E], F32, "gm_wide")
+        for c in range(2):
+            nc.scalar.activation(gm_wide[:, c, :], gm_sb[:, c, 0:1].to_broadcast([P, E]), COPY)
+
+        groups = HALF // BUNDLE
+        sums = [tile([P, groups, PACK], F32, "sums%d" % h) for h in range(2)]
+        means = [tile([P, groups, 1, PACK], F32, "means%d" % h) for h in range(2)]
+        hid_bf = [tile([P, groups, BUNDLE, PACK], BF16, "hid_bf%d" % h) for h in range(2)]
+        hid_codes = [tile([P, HALF], U32, "hid_codes%d" % h) for h in range(2)]
+        hid_scales = [tile([P, HALF], U8, "hid_scales%d" % h) for h in range(2)]
+        p_banks = [[ps.tile([P, HALF], F32, name="p_bank%d%d" % (h, c)) for c in range(2)] for h in range(2)]
+        p_sb = [tile([P, J], F32, "p_sb%d" % c) for c in range(2)]
+
+        for h in range(2):
+            nc.vector.tensor_reduce(
+                out=sums[h][:],
+                in_=a_banks[h][:].rearrange("p t (g s) -> p g t s", s=BUNDLE),
+                axis=mybir.AxisListType.X,
+                op=ALU.add,
+            )
+            nc.scalar.activation(
+                means[h][:].rearrange("p g o t -> p (g o t)"),
+                sums[h][:].rearrange("p g t -> p (g t)"),
+                COPY,
+                scale=1.0 / BUNDLE,
+            )
+        for h in range(2):
+            nc.vector.tensor_tensor(
+                out=hid_bf[h][:],
+                in0=a_banks[h][:].rearrange("p t (g s) -> p g s t", s=BUNDLE),
+                in1=means[h][:].to_broadcast([P, groups, BUNDLE, PACK]),
+                op=ALU.subtract,
+            )
+        for h in range(2):
+            nc.vector.quantize_mx(
+                out=hid_codes[h][:].bitcast(E5M2),
+                scales=hid_scales[h][:],
+                in_=hid_bf[h][:].rearrange("p g s t -> p (g s t)"),
+            )
+            for c in range(2):
+                nc.tensor.matmul_mx(
+                    out=p_banks[h][c][:],
+                    lhsT=wb_sb[:, P * c : P * (c + 1)].bitcast(E5M2),
+                    lhsT_scale=wbs_sb[:, P * c : P * (c + 1)],
+                    rhs=hid_codes[h][:].bitcast(E5M2),
+                    rhs_scale=hid_scales[h][:],
+                    start=True,
+                    stop=True,
+                )
+        nc.scalar.copy(p_sb[0][:, 0:HALF], p_banks[0][0][:])
+        nc.scalar.copy(p_sb[1][:, 0:HALF], p_banks[0][1][:])
+        nc.scalar.copy(p_sb[0][:, HALF:], p_banks[1][0][:])
+        nc.vector.tensor_copy(p_sb[1][:, HALF:], p_banks[1][1][:])
+
+        at_first = tile([P, 2, E], F32, "at_first")
+        at_second = tile([P, 2, E], F32, "at_second")
+        y = tile([P, 2, E], F32, "y")
+        for c in range(2):
+            nc.scalar.activation(at_first[:, c, :], p_sb[c][:].indirect(firsts[:]), COPY)
+        for c in (1, 0):
+            nc.vector.tensor_tensor(at_second[:, c, :], p_sb[c][:].indirect(seconds[:]), gm_wide[:, c, :], ALU.mult)
+        for c in range(2):
+            nc.vector.scalar_tensor_tensor(
+                out=y[:, c, :],
+                in0=at_first[:, c, :],
+                scalar=gm_sb[:, c, 0:1],
+                in1=at_second[:, c, :],
+                op0=ALU.mult,
+                op1=ALU.subtract,
+            )
+        nc.sync.dma_start(out=out.rearrange("(c m) e -> m c e", c=2), in_=y[:])

@@ -23,6 +23,8 @@ PACK = 4
 PASSES = K // (P * PACK)
 HALF = J // 2
 PAD = 8
+GROUPS = HALF // BUNDLE
+SPLIT_FROM = 6
 
 
 def tile_list_steps_levelled_pickgap_kernel(tc, xf, fk, w_words, w_scales, wb_words, wb_scales, gm, offs, offs2, offs3, out):
@@ -31,8 +33,8 @@ def tile_list_steps_levelled_pickgap_kernel(tc, xf, fk, w_words, w_scales, wb_wo
         sb = ctx.enter_context(tc.tile_pool(name="sb", bufs=1))
         ps = ctx.enter_context(tc.psum_pool(name="ps", bufs=1))
 
-        def tile(shape, dtype, name):
-            return sb.tile(shape, dtype, name=name, align_bytes=64)
+        def tile(shape, dtype, name, tag=""):
+            return sb.tile(shape, dtype, name=name, tag=tag or name, align_bytes=64)
 
         slots = tile([P, J // 16], U16, "slots")
         firsts = tile([P, E // 16], U16, "firsts")
@@ -43,32 +45,32 @@ def tile_list_steps_levelled_pickgap_kernel(tc, xf, fk, w_words, w_scales, wb_wo
         w_raw = tile([P, PASSES, 2 * R], U8, "w_raw")
         ws_raw = tile([P, PASSES, R], U8, "ws_raw")
         w_sb = tile([P, PASSES, 2 * R], U8, "w_sb")
-        ws_sb = tile([P, PASSES, R], U8, "ws_sb")
         wb_sb = tile([P, N], U32, "wb_sb")
         wbs_sb = tile([P, N], U8, "wbs_sb")
         picked = [tile([P, PAD + J], F32, "picked%d" % i) for i in range(PASSES * PACK)]
 
-        nc.gpsimd.memset(ws_raw[:].bitcast(I32), 0)
+        zeros = tile([P, PAD], F32, "zeros")
+        nc.vector.memset(zeros[:], 0.0)
         for g in picked:
-            nc.gpsimd.memset(g[:, 0:PAD], 0.0)
-        nc.gpsimd.memset(wbs_sb[:].bitcast(I32), 0)
+            nc.scalar.activation(g[:, 0:PAD], zeros[:], COPY)
+        nc.vector.memset(ws_raw[:].bitcast(I32), 0)
+        for q in range(4):
+            nc.scalar.dma_start(
+                out=ws_raw[32 * q : 32 * q + 4, :, :].bitcast(I32),
+                in_=w_scales[:, 4 * q : 4 * q + 4, :].rearrange("a r c -> r a c").bitcast(I32),
+            )
+        nc.vector.memset(wbs_sb[:].bitcast(I32), 0)
 
         x_rows = xf.rearrange("(a p i) t -> a i p t", a=PASSES, i=PACK)
 
         def load_plane(i):
             nc.sync.dma_start(out=planes[i][:], in_=x_rows[i // PACK, i % PACK])
 
+        nc.sync.dma_start(out=w_raw[:].bitcast(I32), in_=w_words.rearrange("a p c -> p a c").bitcast(I32))
         load_plane(0)
         nc.sync.dma_start(slots[:], offs)
-        nc.sync.dma_start(out=w_raw[:].bitcast(I32), in_=w_words.rearrange("a p c -> p a c").bitcast(I32))
-        load_plane(1)
         nc.sync.dma_start(out=fk_sb[:, :, 0:PACK], in_=fk.rearrange("(a p i) o -> p a (i o)", a=PASSES, i=PACK))
-        for q in range(4):
-            nc.sync.dma_start(
-                out=ws_raw[32 * q : 32 * q + 4, :, :].bitcast(I32),
-                in_=w_scales[:, 4 * q : 4 * q + 4, :].rearrange("a r c -> r a c").bitcast(I32),
-            )
-        for i in range(2, PASSES * PACK):
+        for i in range(1, PASSES * PACK):
             load_plane(i)
         nc.sync.dma_start(out=wb_sb[:].bitcast(I32), in_=wb_words[0].rearrange("p n t -> p (n t)").bitcast(I32))
         for q in range(4):
@@ -86,12 +88,9 @@ def tile_list_steps_levelled_pickgap_kernel(tc, xf, fk, w_words, w_scales, wb_wo
                 out=w_sb[:, a, :].bitcast(U16).rearrange("p (t m) -> p t m", t=PACK),
                 in_=w_raw[:, a, :].bitcast(U16).rearrange("p (m t) -> p t m", t=PACK),
             )
-            nc.vector.tensor_copy(
-                out=ws_sb[:, a, :].rearrange("p (t m) -> p t m", t=PACK),
-                in_=ws_raw[:, a, :].rearrange("p (m t) -> p t m", t=PACK),
-            )
 
         steps = [tile([P, J], F32, "steps%d" % i) for i in range(PASSES * PACK)]
+        ws_sb = []
         u_bf = [tile([P, J, PACK], BF16, "u_bf%d" % a) for a in range(PASSES)]
         u_codes = [tile([P, J], U32, "u_codes%d" % a) for a in range(PASSES)]
         u_scales = [tile([P, J], U8, "u_scales%d" % a) for a in range(PASSES)]
@@ -108,12 +107,20 @@ def tile_list_steps_levelled_pickgap_kernel(tc, xf, fk, w_words, w_scales, wb_wo
                 op1=ALU.add,
             )
             nc.vector.tensor_scalar(
-                out=u_bf[a][:, lo:hi, t],
-                in0=steps[i][:, lo:hi],
+                out=u_bf[a][:, lo:hi, t].rearrange("p (h s g) -> p h s g", g=GROUPS, s=BUNDLE),
+                in0=steps[i][:, lo:hi].rearrange("p (h g s) -> p h s g", g=GROUPS, s=BUNDLE),
                 scalar1=fk_sb[:, a, t : t + 1],
                 scalar2=None,
                 op0=ALU.mult,
             )
+
+        def deal_scales(a, after):
+            dealt = tile([P, R], U8, "ws_sb%d" % a, tag="steps%d" % after)
+            nc.vector.tensor_copy(
+                out=dealt[:].rearrange("p (t m) -> p t m", t=PACK),
+                in_=ws_raw[:, a, :].rearrange("p (m t) -> p t m", t=PACK),
+            )
+            ws_sb.append(dealt)
 
         def first_product(a, h):
             cols = slice(h * HALF, (h + 1) * HALF)
@@ -126,34 +133,31 @@ def tile_list_steps_levelled_pickgap_kernel(tc, xf, fk, w_words, w_scales, wb_wo
                 nc.tensor.matmul_mx(
                     out=a_banks[h][:, t, :],
                     lhsT=w_sb[:, a, 2 * P * t : 2 * P * (t + 1)].bitcast(E2M1),
-                    lhsT_scale=ws_sb[:, a, P * t : P * (t + 1)],
+                    lhsT_scale=ws_sb[a][:, P * t : P * (t + 1)],
                     rhs=u_codes[a][:, cols].bitcast(E4M3),
                     rhs_scale=u_scales[a][:, cols],
                     start=(a == 0 and t == 0),
                     stop=(a == PASSES - 1 and t == PACK - 1),
                 )
 
-        last = PASSES * PACK - 1
-        for i in range(last):
-            nc.scalar.activation(picked[i][:, PAD:], planes[i][:].indirect(slots[:]), COPY)
-            step_and_round(i, 0, J)
-            if i == PACK - 1:
-                first_product(0, 0)
-                first_product(0, 1)
-        nc.vector.tensor_copy(picked[last][:, PAD : PAD + HALF], planes[last][:].indirect(slots[:, 0 : HALF // 16]))
-        nc.scalar.activation(picked[last][:, PAD + HALF :], planes[last][:].indirect(slots[:, HALF // 16 :]), COPY)
-        for h in range(2):
-            step_and_round(last, h * HALF, (h + 1) * HALF)
-            first_product(PASSES - 1, h)
+        for i in range(PASSES * PACK):
+            pieces = [(0, J)] if i < SPLIT_FROM else [(0, HALF), (HALF, J)]
+            for lo, hi in pieces:
+                nc.scalar.activation(picked[i][:, PAD + lo : PAD + hi], planes[i][:].indirect(slots[:, lo // 16 : hi // 16]), COPY)
+            for lo, hi in pieces:
+                step_and_round(i, lo, hi)
+            if i in (2, 3):
+                deal_scales(i - 2, i)
+            if i % PACK == PACK - 1:
+                first_product(i // PACK, 0)
+                first_product(i // PACK, 1)
 
         gm_wide = tile([P, 2, E], F32, "gm_wide")
         for c in range(2):
             nc.scalar.activation(gm_wide[:, c, :], gm_sb[:, c, 0:1].to_broadcast([P, E]), COPY)
 
-        groups = HALF // BUNDLE
-        sums = [tile([P, groups, PACK], F32, "sums%d" % h) for h in range(2)]
-        means = [tile([P, groups, 1, PACK], F32, "means%d" % h) for h in range(2)]
-        hid_bf = [tile([P, groups, BUNDLE, PACK], BF16, "hid_bf%d" % h) for h in range(2)]
+        sums = [tile([P, 1, GROUPS * PACK], F32, "sums%d" % h) for h in range(2)]
+        hid_bf = [tile([P, HALF * PACK], BF16, "hid_bf%d" % h) for h in range(2)]
         hid_codes = [tile([P, HALF], U32, "hid_codes%d" % h) for h in range(2)]
         hid_scales = [tile([P, HALF], U8, "hid_scales%d" % h) for h in range(2)]
         p_banks = [[ps.tile([P, HALF], F32, name="p_bank%d%d" % (h, c)) for c in range(2)] for h in range(2)]
@@ -161,29 +165,25 @@ def tile_list_steps_levelled_pickgap_kernel(tc, xf, fk, w_words, w_scales, wb_wo
 
         for h in range(2):
             nc.vector.tensor_reduce(
-                out=sums[h][:],
-                in_=a_banks[h][:].rearrange("p t (g s) -> p g t s", s=BUNDLE),
+                out=sums[h][:, 0, :].rearrange("p (g t) -> p g t", t=PACK),
+                in_=a_banks[h][:].rearrange("p t (s g) -> p g t s", s=BUNDLE),
                 axis=mybir.AxisListType.X,
                 op=ALU.add,
             )
-            nc.scalar.activation(
-                means[h][:].rearrange("p g o t -> p (g o t)"),
-                sums[h][:].rearrange("p g t -> p (g t)"),
-                COPY,
-                scale=1.0 / BUNDLE,
-            )
         for h in range(2):
-            nc.vector.tensor_tensor(
-                out=hid_bf[h][:],
-                in0=a_banks[h][:].rearrange("p t (g s) -> p g s t", s=BUNDLE),
-                in1=means[h][:].to_broadcast([P, groups, BUNDLE, PACK]),
-                op=ALU.subtract,
+            nc.vector.scalar_tensor_tensor(
+                out=hid_bf[h][:].rearrange("p (s g t) -> p s g t", s=BUNDLE, t=PACK),
+                in0=sums[h][:].to_broadcast([P, BUNDLE, GROUPS * PACK]).rearrange("p s (g t) -> p s g t", t=PACK),
+                scalar=-1.0 / BUNDLE,
+                in1=a_banks[h][:].rearrange("p t (s g) -> p s g t", s=BUNDLE),
+                op0=ALU.mult,
+                op1=ALU.add,
             )
         for h in range(2):
             nc.vector.quantize_mx(
                 out=hid_codes[h][:].bitcast(E5M2),
                 scales=hid_scales[h][:],
-                in_=hid_bf[h][:].rearrange("p g s t -> p (g s t)"),
+                in_=hid_bf[h][:],
             )
             for c in range(2):
                 nc.tensor.matmul_mx(
@@ -195,10 +195,14 @@ def tile_list_steps_levelled_pickgap_kernel(tc, xf, fk, w_words, w_scales, wb_wo
                     start=True,
                     stop=True,
                 )
-        nc.scalar.copy(p_sb[0][:, 0:HALF], p_banks[0][0][:])
-        nc.scalar.copy(p_sb[1][:, 0:HALF], p_banks[0][1][:])
-        nc.scalar.copy(p_sb[0][:, HALF:], p_banks[1][0][:])
-        nc.vector.tensor_copy(p_sb[1][:, HALF:], p_banks[1][1][:])
+        for h in range(2):
+            for c in range(2):
+                in_slot_order = p_banks[h][c][:].rearrange("p (s g) -> p g s", s=BUNDLE)
+                dst = p_sb[c][:, h * HALF : (h + 1) * HALF].rearrange("p (g s) -> p g s", s=BUNDLE)
+                if h == 1 and c == 1:
+                    nc.vector.tensor_copy(dst, in_slot_order)
+                else:
+                    nc.scalar.copy(dst, in_slot_order)
 
         at_first = tile([P, 2, E], F32, "at_first")
         at_second = tile([P, 2, E], F32, "at_second")

@@ -23,8 +23,8 @@ PACK = 4
 PASSES = K // (P * PACK)
 HALF = J // 2
 PAD = 8
+HOLD = 5
 GROUPS = HALF // BUNDLE
-SPLIT_FROM = 6
 
 
 def tile_list_steps_levelled_pickgap_kernel(tc, xf, fk, w_words, w_scales, wb_words, wb_scales, gm, offs, offs2, offs3, out):
@@ -89,17 +89,19 @@ def tile_list_steps_levelled_pickgap_kernel(tc, xf, fk, w_words, w_scales, wb_wo
                 in_=w_raw[:, a, :].bitcast(U16).rearrange("p (m t) -> p t m", t=PACK),
             )
 
-        steps = [tile([P, J], F32, "steps%d" % i) for i in range(PASSES * PACK)]
         ws_sb = []
         u_bf = [tile([P, J, PACK], BF16, "u_bf%d" % a) for a in range(PASSES)]
-        u_codes = [tile([P, J], U32, "u_codes%d" % a) for a in range(PASSES)]
+        u_codes = []
         u_scales = [tile([P, J], U8, "u_scales%d" % a) for a in range(PASSES)]
         a_banks = [ps.tile([P, PACK, HALF], F32, name="a_bank%d" % h) for h in range(2)]
 
         def step_and_round(i, lo, hi):
             a, t = divmod(i, PACK)
+            base = lo - lo % HALF
+            place = lo if i < PASSES * PACK - 1 else lo - base
+            steps = tile([P, hi - lo], F32, "steps%d_%d" % (i, lo), tag="steps%d_%d" % (i, place))
             nc.vector.scalar_tensor_tensor(
-                out=steps[i][:, lo:hi],
+                out=steps[:],
                 in0=picked[i][:, PAD - 1 + lo : PAD - 1 + hi],
                 scalar=-0.6,
                 in1=picked[i][:, PAD + lo : PAD + hi],
@@ -107,15 +109,15 @@ def tile_list_steps_levelled_pickgap_kernel(tc, xf, fk, w_words, w_scales, wb_wo
                 op1=ALU.add,
             )
             nc.vector.tensor_scalar(
-                out=u_bf[a][:, lo:hi, t].rearrange("p (h s g) -> p h s g", g=GROUPS, s=BUNDLE),
-                in0=steps[i][:, lo:hi].rearrange("p (h g s) -> p h s g", g=GROUPS, s=BUNDLE),
+                out=u_bf[a][:, base : base + HALF, t].rearrange("p (s g) -> p s g", s=BUNDLE)[:, :, (lo - base) // BUNDLE : (hi - base) // BUNDLE],
+                in0=steps[:].rearrange("p (g s) -> p s g", s=BUNDLE),
                 scalar1=fk_sb[:, a, t : t + 1],
                 scalar2=None,
                 op0=ALU.mult,
             )
 
         def deal_scales(a, after):
-            dealt = tile([P, R], U8, "ws_sb%d" % a, tag="steps%d" % after)
+            dealt = tile([P, R], U8, "ws_sb%d" % a, tag="picked%d" % after)
             nc.vector.tensor_copy(
                 out=dealt[:].rearrange("p (t m) -> p t m", t=PACK),
                 in_=ws_raw[:, a, :].rearrange("p (m t) -> p t m", t=PACK),
@@ -141,16 +143,34 @@ def tile_list_steps_levelled_pickgap_kernel(tc, xf, fk, w_words, w_scales, wb_wo
                 )
 
         for i in range(PASSES * PACK):
-            pieces = [(0, J)] if i < SPLIT_FROM else [(0, HALF), (HALF, J)]
+            cuts = [0, HALF, J] if i < PASSES * PACK - 1 else [0, HALF // 2, HALF, J]
+            pieces = list(zip(cuts[:-1], cuts[1:]))
             for lo, hi in pieces:
                 nc.scalar.activation(picked[i][:, PAD + lo : PAD + hi], planes[i][:].indirect(slots[:, lo // 16 : hi // 16]), COPY)
-            for lo, hi in pieces:
-                step_and_round(i, lo, hi)
-            if i in (2, 3):
-                deal_scales(i - 2, i)
-            if i % PACK == PACK - 1:
-                first_product(i // PACK, 0)
-                first_product(i // PACK, 1)
+            for h in range(2):
+                for lo, hi in pieces:
+                    if lo // HALF == h:
+                        step_and_round(i, lo, hi)
+                if h == 1 and i in (2, 3):
+                    deal_scales(i - 2, i)
+                if i == PASSES * PACK - 1:
+                    if h == 0:
+                        u_codes.append(tile([P, J], U32, "u_codes1"))
+                    first_product(1, h)
+            if i == HOLD:
+                u_codes.append(tile([P, J], U32, "u_codes0", tag="plane%d" % HOLD))
+                first_product(0, 0)
+                warm = ps.tile([P, R], F32, name="warm")
+                nc.tensor.matmul_mx(
+                    out=warm[:],
+                    lhsT=u_codes[0][:, 0:P].bitcast(E4M3),
+                    lhsT_scale=u_scales[0][:, 0:P],
+                    rhs=w_sb[:, 0, :].bitcast(E2M1),
+                    rhs_scale=ws_sb[0][:],
+                    start=True,
+                    stop=True,
+                )
+                first_product(0, 1)
 
         gm_wide = tile([P, 2, E], F32, "gm_wide")
         for c in range(2):

from contextlib import ExitStack

import concourse.mybir as mybir

K, T, J, R, N, E = 1024, 1024, 256, 512, 256, 64
BUNDLE = 8
FLOPS = 2 * K * R * J + 2 * R * N * J

F32 = mybir.dt.float32
BF16 = mybir.dt.bfloat16
I32 = mybir.dt.int32
U32 = mybir.dt.uint32
U16 = mybir.dt.uint16
U8 = mybir.dt.uint8
E4M3 = mybir.dt.float8_e4m3fn_x4
E5M2 = mybir.dt.float8_e5m2_x4
E2M1 = mybir.dt.float4_e2m1fn_x4
ALU = mybir.AluOpType
COPY = mybir.ActivationFunctionType.Copy

P = 128
PACK = 4
PASSES = K // (P * PACK)
HALF = J // 2
PAD = 8
HOLD = 5
GROUPS = HALF // BUNDLE


def tile_list_steps_levelled_pickgap_kernel(tc, xf, fk, w_words, w_scales, wb_words, wb_scales, gm, offs, offs2, offs3, out):
    nc = tc.nc
    with ExitStack() as ctx:
        sb = ctx.enter_context(tc.tile_pool(name="sb", bufs=1))
        ps = ctx.enter_context(tc.psum_pool(name="ps", bufs=1))

        def tile(shape, dtype, name, tag=""):
            return sb.tile(shape, dtype, name=name, tag=tag or name, align_bytes=64)

        slots = tile([P, J // 16], U16, "slots")
        firsts = tile([P, E // 16], U16, "firsts")
        seconds = tile([P, E // 16], U16, "seconds")
        planes = [tile([P, T], F32, "plane%d" % i) for i in range(PASSES * PACK)]
        fk_sb = tile([P, PASSES, 8], F32, "fk_sb")
        gm_sb = tile([P, 2, 8], F32, "gm_sb")
        w_raw = tile([P, PASSES, 2 * R], U8, "w_raw")
        ws_raw = tile([P, PASSES, R], U8, "ws_raw")
        w_sb = tile([P, PASSES, 2 * R], U8, "w_sb")
        wb_sb = tile([P, N], U32, "wb_sb")
        wbs_sb = tile([P, N], U8, "wbs_sb")
        picked = [tile([P, PAD + J], F32, "picked%d" % i) for i in range(PASSES * PACK)]

        zeros = tile([P, PAD], F32, "zeros")
        nc.vector.memset(zeros[:], 0.0)
        for g in picked:
            nc.scalar.activation(g[:, 0:PAD], zeros[:], COPY)
        nc.vector.memset(ws_raw[:].bitcast(I32), 0)
        for q in range(4):
            nc.scalar.dma_start(
                out=ws_raw[32 * q : 32 * q + 4, :, :].bitcast(I32),
                in_=w_scales[:, 4 * q : 4 * q + 4, :].rearrange("a r c -> r a c").bitcast(I32),
            )
        nc.vector.memset(wbs_sb[:].bitcast(I32), 0)

        x_rows = xf.rearrange("(a p i) t -> a i p t", a=PASSES, i=PACK)

        def load_plane(i):
            nc.sync.dma_start(out=planes[i][:], in_=x_rows[i // PACK, i % PACK])

        nc.sync.dma_start(out=w_raw[:].bitcast(I32), in_=w_words.rearrange("a p c -> p a c").bitcast(I32))
        load_plane(0)
        nc.sync.dma_start(slots[:], offs)
        nc.sync.dma_start(out=fk_sb[:, :, 0:PACK], in_=fk.rearrange("(a p i) o -> p a (i o)", a=PASSES, i=PACK))
        for i in range(1, PASSES * PACK):
            load_plane(i)
        nc.sync.dma_start(out=wb_sb[:].bitcast(I32), in_=wb_words[0].rearrange("p n t -> p (n t)").bitcast(I32))
        for q in range(4):
            nc.sync.dma_start(
                out=wbs_sb[32 * q : 32 * q + 4, :].bitcast(I32),
                in_=wb_scales[0, 4 * q : 4 * q + 4, :].bitcast(I32),
            )
        with nc.allow_non_contiguous_dma(reason="one factor a partition"):
            nc.sync.dma_start(out=gm_sb[:, :, 0:1], in_=gm.rearrange("(c m) o -> m c o", c=2))
        nc.sync.dma_start(firsts[:], offs2)
        nc.sync.dma_start(seconds[:], offs3)

        for a in range(PASSES):
            nc.vector.tensor_copy(
                out=w_sb[:, a, :].bitcast(U16).rearrange("p (t m) -> p t m", t=PACK),
                in_=w_raw[:, a, :].bitcast(U16).rearrange("p (m t) -> p t m", t=PACK),
            )

        ws_sb = []
        u_bf = [tile([P, J, PACK], BF16, "u_bf%d" % a) for a in range(PASSES)]
        u_codes = []
        u_scales = [tile([P, J], U8, "u_scales%d" % a) for a in range(PASSES)]
        a_banks = [ps.tile([P, PACK, HALF], F32, name="a_bank%d" % h) for h in range(2)]

        def step_and_round(i, lo, hi):
            a, t = divmod(i, PACK)
            base = lo - lo % HALF
            place = lo if i < PASSES * PACK - 1 else lo - base
            steps = tile([P, hi - lo], F32, "steps%d_%d" % (i, lo), tag="steps%d_%d" % (i, place))
            nc.vector.scalar_tensor_tensor(
                out=steps[:],
                in0=picked[i][:, PAD - 1 + lo : PAD - 1 + hi],
                scalar=-0.6,
                in1=picked[i][:, PAD + lo : PAD + hi],
                op0=ALU.mult,
                op1=ALU.add,
            )
            nc.vector.tensor_scalar(
                out=u_bf[a][:, base : base + HALF, t].rearrange("p (s g) -> p s g", s=BUNDLE)[:, :, (lo - base) // BUNDLE : (hi - base) // BUNDLE],
                in0=steps[:].rearrange("p (g s) -> p s g", s=BUNDLE),
                scalar1=fk_sb[:, a, t : t + 1],
                scalar2=None,
                op0=ALU.mult,
            )

        def deal_scales(a, after):
            dealt = tile([P, R], U8, "ws_sb%d" % a, tag="picked%d" % after)
            nc.vector.tensor_copy(
                out=dealt[:].rearrange("p (t m) -> p t m", t=PACK),
                in_=ws_raw[:, a, :].rearrange("p (m t) -> p t m", t=PACK),
            )
            ws_sb.append(dealt)

        def first_product(a, h):
            cols = slice(h * HALF, (h + 1) * HALF)
            nc.vector.quantize_mx(
                out=u_codes[a][:, cols].bitcast(E4M3),
                scales=u_scales[a][:, cols],
                in_=u_bf[a][:, cols, :].rearrange("p j t -> p (j t)"),
            )
            for t in range(PACK):
                nc.tensor.matmul_mx(
                    out=a_banks[h][:, t, :],
                    lhsT=w_sb[:, a, 2 * P * t : 2 * P * (t + 1)].bitcast(E2M1),
                    lhsT_scale=ws_sb[a][:, P * t : P * (t + 1)],
                    rhs=u_codes[a][:, cols].bitcast(E4M3),
                    rhs_scale=u_scales[a][:, cols],
                    start=(a == 0 and t == 0),
                    stop=(a == PASSES - 1 and t == PACK - 1),
                )

        for i in range(PASSES * PACK):
            cuts = [0, HALF, J] if i < PASSES * PACK - 1 else [0, HALF // 2, HALF, J]
            pieces = list(zip(cuts[:-1], cuts[1:]))
            for lo, hi in pieces:
                nc.scalar.activation(picked[i][:, PAD + lo : PAD + hi], planes[i][:].indirect(slots[:, lo // 16 : hi // 16]), COPY)
            for h in range(2):
                for lo, hi in pieces:
                    if lo // HALF == h:
                        step_and_round(i, lo, hi)
                if h == 1 and i in (2, 3):
                    deal_scales(i - 2, i)
                if i == PASSES * PACK - 1:
                    if h == 0:
                        u_codes.append(tile([P, J], U32, "u_codes1"))
                    first_product(1, h)
            if i == HOLD:
                u_codes.append(tile([P, J], U32, "u_codes0", tag="plane%d" % HOLD))
                first_product(0, 0)
                warm = ps.tile([P, R], F32, name="warm")
                nc.tensor.matmul_mx(
                    out=warm[:],
                    lhsT=u_codes[0][:, 0:P].bitcast(E4M3),
                    lhsT_scale=u_scales[0][:, 0:P],
                    rhs=w_sb[:, 0, :].bitcast(E2M1),
                    rhs_scale=ws_sb[0][:],
                    start=True,
                    stop=True,
                )
                first_product(0, 1)

        gm_wide = tile([P, 2, E], F32, "gm_wide")
        for c in range(2):
            nc.scalar.activation(gm_wide[:, c, :], gm_sb[:, c, 0:1].to_broadcast([P, E]), COPY)

        sums = [tile([P, 1, GROUPS * PACK], F32, "sums%d" % h) for h in range(2)]
        hid_bf = [tile([P, HALF * PACK], BF16, "hid_bf%d" % h) for h in range(2)]
        hid_codes = [tile([P, HALF], U32, "hid_codes%d" % h) for h in range(2)]
        hid_scales = [tile([P, HALF], U8, "hid_scales%d" % h) for h in range(2)]
        p_banks = [[ps.tile([P, HALF], F32, name="p_bank%d%d" % (h, c)) for c in range(2)] for h in range(2)]
        p_sb = [tile([P, J], F32, "p_sb%d" % c) for c in range(2)]

        for h in range(2):
            nc.vector.tensor_reduce(
                out=sums[h][:, 0, :].rearrange("p (g t) -> p g t", t=PACK),
                in_=a_banks[h][:].rearrange("p t (s g) -> p g t s", s=BUNDLE),
                axis=mybir.AxisListType.X,
                op=ALU.add,
            )
        for h in range(2):
            nc.vector.scalar_tensor_tensor(
                out=hid_bf[h][:].rearrange("p (s g t) -> p s g t", s=BUNDLE, t=PACK),
                in0=sums[h][:].to_broadcast([P, BUNDLE, GROUPS * PACK]).rearrange("p s (g t) -> p s g t", t=PACK),
                scalar=-1.0 / BUNDLE,
                in1=a_banks[h][:].rearrange("p t (s g) -> p s g t", s=BUNDLE),
                op0=ALU.mult,
                op1=ALU.add,
            )
        for h in range(2):
            nc.vector.quantize_mx(
                out=hid_codes[h][:].bitcast(E5M2),
                scales=hid_scales[h][:],
                in_=hid_bf[h][:],
            )
            for c in range(2):
                nc.tensor.matmul_mx(
                    out=p_banks[h][c][:],
                    lhsT=wb_sb[:, P * c : P * (c + 1)].bitcast(E5M2),
                    lhsT_scale=wbs_sb[:, P * c : P * (c + 1)],
                    rhs=hid_codes[h][:].bitcast(E5M2),
                    rhs_scale=hid_scales[h][:],
                    start=True,
                    stop=True,
                )
        for h in range(2):
            for c in range(2):
                in_slot_order = p_banks[h][c][:].rearrange("p (s g) -> p g s", s=BUNDLE)
                dst = p_sb[c][:, h * HALF : (h + 1) * HALF].rearrange("p (g s) -> p g s", s=BUNDLE)
                if h == 1 and c == 1:
                    nc.vector.tensor_copy(dst, in_slot_order)
                else:
                    nc.scalar.copy(dst, in_slot_order)

        at_first = tile([P, 2, E], F32, "at_first")
        at_second = tile([P, 2, E], F32, "at_second")
        y = tile([P, 2, E], F32, "y")
        for c in range(2):
            nc.scalar.activation(at_first[:, c, :], p_sb[c][:].indirect(firsts[:]), COPY)
        for c in (1, 0):
            nc.vector.tensor_tensor(at_second[:, c, :], p_sb[c][:].indirect(seconds[:]), gm_wide[:, c, :], ALU.mult)
        for c in range(2):
            nc.vector.scalar_tensor_tensor(
                out=y[:, c, :],
                in0=at_first[:, c, :],
                scalar=gm_sb[:, c, 0:1],
                in1=at_second[:, c, :],
                op0=ALU.mult,
                op1=ALU.subtract,
            )
        nc.sync.dma_start(out=out.rearrange("(c m) e -> m c e", c=2), in_=y[:])
